import numpy as np
import ml_dtypes


def mxq(x, axis, fmt="e4m3"):
    dtype, down = {"e4m3": (ml_dtypes.float8_e4m3fn, 7), "e5m2": (ml_dtypes.float8_e5m2, 14)}[fmt]
    v = np.moveaxis(np.asarray(x, np.float32).astype(ml_dtypes.bfloat16).astype(np.float64), axis, -1)
    blocks = v.reshape(v.shape[:-1] + (-1, 32))
    amax = np.abs(blocks).max(-1, keepdims=True)
    byte = np.maximum(np.where(amax > 0, np.frexp(amax)[1] - 1 + 127, 0) - down, 1)
    scale = np.exp2(byte - 127.0)
    codes = (blocks / scale).astype(np.float32).astype(dtype).astype(np.float64)
    return np.moveaxis((codes * scale).reshape(v.shape), -1, axis)


WIDE = False


def mx_kscale(k):
    if not WIDE:
        return np.ones(k)
    levels = np.array([24, -24, 12, -12, 0])
    if k % 512:
        return np.exp2(np.random.permutation(np.resize(levels, k // 32))).repeat(32)
    a = np.empty((k // 512, 16))
    for p in range(k // 512):
        a[p, :8] = np.random.permutation(np.resize(levels, 8))
        for g in range(8):
            far = levels[np.abs(levels - a[p, g]) >= 10]
            a[p, g + 8] = far[np.random.randint(len(far))]
    return np.exp2(a.ravel()).repeat(32)


def f64(x):
    return np.asarray(x).astype(np.float64)


def striped(idx):
    return np.tile(idx.reshape(-1, 16).T, (8, 1)).astype(np.uint16)


def unstriped(offs):
    return offs[:16].T.reshape(-1).astype(np.int64)


E2M1 = np.array([0.0, 0.5, 1.0, 1.5, 2.0, 3.0, 4.0, 6.0, -0.0, -0.5, -1.0, -1.5, -2.0, -3.0, -4.0, -6.0])


def pack_weight(w, fmt):
    k, n = w.shape
    w = f64(np.asarray(w, np.float32).astype(ml_dtypes.bfloat16)).reshape(k // 32, 32, n)
    amax = np.abs(w).max(1)
    if fmt == "e4m3":
        byte = np.frexp(amax)[1] - 1 + 127 - 7
    else:
        mant, ex = np.frexp(amax / 6.0)
        byte = np.where(mant > 0.5, ex, ex - 1) + 127
    byte = np.clip(np.where(amax > 0, byte, 1), 1, 254)
    scaled = (w * np.exp2(127.0 - byte)[:, None, :]).reshape(k, n).astype(np.float32)
    by_word = np.ascontiguousarray(scaled.reshape(k // 512, 128, 4, n).transpose(0, 1, 3, 2))
    if fmt == "e4m3":
        words = by_word.astype(ml_dtypes.float8_e4m3fn).view(np.uint8)
    else:
        c = by_word.astype(ml_dtypes.float4_e2m1fn).view(np.uint8) & 0xF
        words = (c[..., 0::2] | (c[..., 1::2] << 4)).reshape(k // 512, 128, 2 * n)
    return np.ascontiguousarray(words), np.ascontiguousarray(byte.astype(np.uint8).reshape(k // 512, 16, n))


def unpack_weight(words, scales, fmt):
    g, _, n = scales.shape
    words = np.ascontiguousarray(words).reshape(g, 128, n, -1)
    if fmt == "e4m3":
        vals = words.view(ml_dtypes.float8_e4m3fn).astype(np.float64)
    else:
        nib = np.empty((g, 128, n, 4), np.uint8)
        nib[..., 0::2] = words & 0xF
        nib[..., 1::2] = words >> 4
        vals = E2M1[nib]
    vals = vals * np.repeat(np.exp2(scales.astype(np.float64) - 127.0), 8, axis=1)[..., None]
    return vals.transpose(0, 1, 3, 2).reshape(g * 512, n)


def pack_table4(v):
    words, scales = pack_weight(v, "e2m1")
    g, t = words.shape[0] // 2, v.shape[1]
    return np.ascontiguousarray(words.reshape(g, 2, 128, t, 2).transpose(0, 2, 3, 1, 4).reshape(g, 128, t, 4)), scales


def unpack_table4(words, scales):
    g, _, t, _ = words.shape
    return unpack_weight(words.reshape(g, 128, t, 2, 2).transpose(0, 3, 1, 2, 4).reshape(2 * g, 128, 2 * t), scales, "e2m1")


K, N, T, J = 1024, 256, 1024, 512


def setup_inputs():
    n = np.random.standard_normal
    s = mx_kscale(K)[:, None]
    p_tab = pack_table4(n((K, T)) * s)
    p_wk4 = pack_weight(n((K, N)) / np.sqrt(K) / s, "e2m1")
    return {
        "tab_words": p_tab[0],
        "tab_scales": p_tab[1],
        "wk4_words": p_wk4[0],
        "wk4_scales": p_wk4[1],
        "wkd": (0.4 * (n((K, N)) / np.sqrt(K) / s)).astype(np.float32),
        "wv": (n((K, N)) / np.sqrt(K) / s).astype(np.float32),
        "st": (n((N, J))).astype(np.float32),
        "rT": (n((N, T))).astype(np.float32),
        "offs": striped(np.random.permutation(T)[:J]),
    }


def reference(tab_words, tab_scales, wk4_words, wk4_scales, wkd, wv, st, rT, offs):
    idx = unstriped(offs)
    tab_ = unpack_table4(tab_words, tab_scales)[:, idx]
    wk4_ = unpack_weight(wk4_words, wk4_scales, "e2m1")
    wkd_ = mxq(f64(wkd), 0, "e4m3")
    wv_ = mxq(f64(wv), 0, "e4m3")
    ke = wk4_.T @ tab_ + wkd_.T @ tab_
    ve = wv_.T @ tab_
    gate = np.tanh(ke * f64(st))
    return f64(rT)[:, idx] + gate * ve

@@ -1,0 +1,154 @@
+from contextlib import ExitStack
+
+import concourse.mybir as mybir
+
+K, N, T, J = 1024, 256, 1024, 512
+FLOPS = 3 * 2 * K * N * J
+
+F32 = mybir.dt.float32
+BF16 = mybir.dt.bfloat16
+I32 = mybir.dt.int32
+U32 = mybir.dt.uint32
+U16 = mybir.dt.uint16
+U8 = mybir.dt.uint8
+FP8X4 = mybir.dt.float8_e4m3fn_x4
+FP4X4 = mybir.dt.float4_e2m1fn_x4
+MULT = mybir.AluOpType.mult
+ADD = mybir.AluOpType.add
+COPY = mybir.ActivationFunctionType.Copy
+TANH = mybir.ActivationFunctionType.Tanh
+
+P = 128
+PACK = 4
+K_PASS = P * PACK
+PASSES = K // K_PASS
+HALVES = N // P
+QUADS = 4
+
+
+def tile_list_engram_dl_tanhL_kernel(
+    tc, tab_words, tab_scales, wk4_words, wk4_scales, wkd, wv, st, rT, offs, out
+):
+    nc = tc.nc
+    with ExitStack() as ctx:
+        lists = ctx.enter_context(tc.tile_pool(name="lists", bufs=1))
+        keep = ctx.enter_context(tc.tile_pool(name="keep", bufs=1))
+        psum = ctx.enter_context(tc.psum_pool(name="psum", bufs=1))
+
+        offsets = lists.tile([P, J // 16], U16, name="offsets")
+        nc.sync.dma_start(offsets[:], offs)
+
+        tscale = keep.tile([P, PASSES, T], U8, name="tscale", align_bytes=64)
+        nc.gpsimd.memset(tscale[:].bitcast(I32), 0)
+        w4scale = keep.tile([P, PASSES, N], U8, name="w4scale", align_bytes=64)
+        nc.gpsimd.memset(w4scale[:].bitcast(I32), 0)
+        twords = keep.tile([P, T], I32, name="twords", align_bytes=64)
+        nc.sync.dma_start(twords[:], tab_words[0].rearrange("p t b -> p (t b)").bitcast(I32))
+        for q in range(QUADS):
+            nc.scalar.dma_start(
+                tscale[32 * q : 32 * q + 4, :, :].bitcast(I32),
+                tab_scales[:, 4 * q : 4 * q + 4, :].rearrange("a r t -> r a t").bitcast(I32),
+            )
+
+        raw = {}
+
+        def load_weight(name, w, a):
+            raw[name, a] = keep.tile([P, PACK, N], F32, name="raw_%s%d" % (name, a), align_bytes=64)
+            nc.sync.dma_start(
+                raw[name, a][:], w[a * K_PASS : (a + 1) * K_PASS, :].rearrange("(p t) n -> p t n", t=PACK)
+            )
+
+        load_weight("kd", wkd, 0)
+        load_weight("kd", wkd, 1)
+        w4words = keep.tile([P, PASSES, 2 * N], U8, name="w4words", align_bytes=64)
+        nc.sync.dma_start(w4words[:].bitcast(I32), wk4_words.rearrange("a p b -> p a b").bitcast(I32))
+        for q in range(QUADS):
+            nc.sync.dma_start(
+                w4scale[32 * q : 32 * q + 4, :, :].bitcast(I32),
+                wk4_scales[:, 4 * q : 4 * q + 4, :].rearrange("a r n -> r a n").bitcast(I32),
+            )
+        load_weight("v", wv, 0)
+        load_weight("v", wv, 1)
+        state = []
+        for h in range(HALVES):
+            state.append(keep.tile([P, J], F32, name="state%d" % h, align_bytes=64))
+            nc.sync.dma_start(state[h][:], st[h * P : (h + 1) * P, :])
+        record = []
+        for h in range(HALVES):
+            record.append(keep.tile([P, T], F32, name="record%d" % h, align_bytes=64))
+            nc.sync.dma_start(record[h][:], rT[h * P : (h + 1) * P, :])
+
+        gwords = keep.tile([P, J], U32, name="gwords", align_bytes=64)
+        codes = [keep.tile([P, J], U16, name="tcodes%d" % a, align_bytes=64) for a in range(PASSES)]
+        planes = [keep.tile([P, J], U8, name="gscale%d" % a, align_bytes=64) for a in range(PASSES)]
+
+        def table_pass(a):
+            nc.vector.tensor_copy(planes[a][:], tscale[:, a, :].indirect(offsets[:]))
+            nc.vector.tensor_copy(codes[a][:], gwords[:].bitcast(U16).rearrange("p (j d) -> p d j", d=2)[:, a, :])
+
+        nc.vector.tensor_copy(gwords[:], twords[:].bitcast(U32).indirect(offsets[:]))
+
+        ke = [psum.tile([P, J], F32, name="ke%d" % h) for h in range(HALVES)]
+        ve = [psum.tile([P, J], F32, name="ve%d" % h) for h in range(HALVES)]
+
+        def product(acc, lhs, lhs_scale, a, start, stop):
+            nc.tensor.matmul_mx(
+                out=acc[:], lhsT=lhs, lhsT_scale=lhs_scale,
+                rhs=codes[a][:].bitcast(FP4X4), rhs_scale=planes[a][:], start=start, stop=stop,
+            )
+
+        def cast(name, a, h, on_vector):
+            grouped = keep.tile([P, P, PACK], BF16, name="grp_%s%d%d" % (name, a, h), align_bytes=64)
+            dst = grouped[:].rearrange("p (c i) t -> p c t i", i=4)
+            src = raw[name, a][:, :, h * P : (h + 1) * P].rearrange("p t (c i) -> p c t i", i=4)
+            if on_vector:
+                nc.vector.tensor_copy(dst, src)
+            else:
+                nc.scalar.activation(dst, src, COPY)
+            return grouped
+
+        def quantise(name, a, h, grouped):
+            wcodes = keep.tile([P, P], U32, name="wc_%s%d%d" % (name, a, h), align_bytes=64)
+            wscale = keep.tile([P, P], U8, name="ws_%s%d%d" % (name, a, h), align_bytes=64)
+            nc.vector.quantize_mx(
+                out=wcodes[:].bitcast(FP8X4), scales=wscale[:], in_=grouped[:].rearrange("p n t -> p (n t)")
+            )
+            return wcodes, wscale
+
+        def base_product(a, h, stop):
+            product(
+                ke[h], w4words[:, a, 2 * P * h : 2 * P * (h + 1)].bitcast(FP4X4),
+                w4scale[:, a, h * P : (h + 1) * P], a, False, stop,
+            )
+
+        for name, acc in (("kd", ke), ("v", ve)):
+            for a in range(PASSES):
+                grouped = [cast(name, a, h, h == 1 and (name, a) == ("v", 1)) for h in range(HALVES)]
+                if name == "kd":
+                    table_pass(a)
+                    if a == 1:
+                        for h in range(HALVES):
+                            base_product(a, h, False)
+                for h in range(HALVES):
+                    wcodes, wscale = quantise(name, a, h, grouped[h])
+                    product(acc[h], wcodes[:].bitcast(FP8X4), wscale[:], a, a == 0, a == PASSES - 1)
+                if name == "kd" and a == 0:
+                    for h in range(HALVES):
+                        base_product(a, h, False)
+
+        gate = []
+        for h in range(HALVES):
+            pre = keep.tile([P, J], F32, name="pre%d" % h, align_bytes=64)
+            nc.vector.tensor_tensor(pre[:], ke[h][:], state[h][:], MULT)
+            gate.append(keep.tile([P, J], F32, name="gate%d" % h, align_bytes=64))
+            nc.scalar.activation(gate[h][:], pre[:], TANH)
+        for h in range(HALVES):
+            gated = keep.tile([P, J], F32, name="gated%d" % h, align_bytes=64)
+            nc.vector.tensor_tensor(gated[:], ve[h][:], gate[h][:], MULT)
+            for c in range(2):
+                cols = slice(c * J // 2, (c + 1) * J // 2)
+                res = keep.tile([P, J // 2], F32, name="res%d%d" % (h, c), align_bytes=64)
+                nc.vector.tensor_tensor(
+                    res[:], record[h][:].indirect(offsets[:, c * J // 32 : (c + 1) * J // 32]), gated[:, cols], ADD
+                )
+                nc.sync.dma_start(out[h * P : (h + 1) * P, cols], res[:])

@@ -39,13 +39,17 @@ def tile_list_engram_dl_tanhL_kernel(
         nc.sync.dma_start(offsets[:], offs)
 
         tscale = keep.tile([P, PASSES, T], U8, name="tscale", align_bytes=64)
-        nc.gpsimd.memset(tscale[:].bitcast(I32), 0)
+        cleared = tscale[:].rearrange("p a t -> p (a t)").bitcast(I32)
+        nc.gpsimd.memset(cleared[:, :320], 0)
+        nc.vector.memset(cleared[:, 320:], 0)
         w4scale = keep.tile([P, PASSES, N], U8, name="w4scale", align_bytes=64)
         nc.gpsimd.memset(w4scale[:].bitcast(I32), 0)
         twords = keep.tile([P, T], I32, name="twords", align_bytes=64)
         nc.sync.dma_start(twords[:], tab_words[0].rearrange("p t b -> p (t b)").bitcast(I32))
+        w4words = keep.tile([P, PASSES, 2 * N], U8, name="w4words", align_bytes=64)
+        nc.sync.dma_start(w4words[:].bitcast(I32), wk4_words.rearrange("a p b -> p a b").bitcast(I32))
         for q in range(QUADS):
-            nc.scalar.dma_start(
+            nc.sync.dma_start(
                 tscale[32 * q : 32 * q + 4, :, :].bitcast(I32),
                 tab_scales[:, 4 * q : 4 * q + 4, :].rearrange("a r t -> r a t").bitcast(I32),
             )
@@ -53,21 +57,19 @@ def tile_list_engram_dl_tanhL_kernel(
         raw = {}
 
         def load_weight(name, w, a):
-            raw[name, a] = keep.tile([P, PACK, N], F32, name="raw_%s%d" % (name, a), align_bytes=64)
+            raw[name, a] = keep.tile([P, PACK, N], F32, name="raw_%s%d" % (name, a), tag="raw_%s%d" % (name, a), align_bytes=64)
             nc.sync.dma_start(
                 raw[name, a][:], w[a * K_PASS : (a + 1) * K_PASS, :].rearrange("(p t) n -> p t n", t=PACK)
             )
 
         load_weight("kd", wkd, 0)
         load_weight("kd", wkd, 1)
-        w4words = keep.tile([P, PASSES, 2 * N], U8, name="w4words", align_bytes=64)
-        nc.sync.dma_start(w4words[:].bitcast(I32), wk4_words.rearrange("a p b -> p a b").bitcast(I32))
+        load_weight("v", wv, 0)
         for q in range(QUADS):
             nc.sync.dma_start(
                 w4scale[32 * q : 32 * q + 4, :, :].bitcast(I32),
                 wk4_scales[:, 4 * q : 4 * q + 4, :].rearrange("a r n -> r a n").bitcast(I32),
             )
-        load_weight("v", wv, 0)
         load_weight("v", wv, 1)
         state = []
         for h in range(HALVES):
@@ -79,14 +81,16 @@ def tile_list_engram_dl_tanhL_kernel(
             nc.sync.dma_start(record[h][:], rT[h * P : (h + 1) * P, :])
 
         gwords = keep.tile([P, J], U32, name="gwords", align_bytes=64)
-        codes = [keep.tile([P, J], U16, name="tcodes%d" % a, align_bytes=64) for a in range(PASSES)]
-        planes = [keep.tile([P, J], U8, name="gscale%d" % a, align_bytes=64) for a in range(PASSES)]
+        codes = keep.tile([P, PASSES, J], U16, name="tcodes", align_bytes=64)
+        planes = {}
 
         def table_pass(a):
+            tag = "raw_kd0" if a == 1 else "gscale0"
+            planes[a] = keep.tile([P, J], U8, name="gscale%d" % a, tag=tag, align_bytes=64)
             nc.vector.tensor_copy(planes[a][:], tscale[:, a, :].indirect(offsets[:]))
-            nc.vector.tensor_copy(codes[a][:], gwords[:].bitcast(U16).rearrange("p (j d) -> p d j", d=2)[:, a, :])
 
         nc.vector.tensor_copy(gwords[:], twords[:].bitcast(U32).indirect(offsets[:]))
+        nc.vector.tensor_copy(codes[:], gwords[:].bitcast(U16).rearrange("p (j d) -> p d j", d=2))
 
         ke = [psum.tile([P, J], F32, name="ke%d" % h) for h in range(HALVES)]
         ve = [psum.tile([P, J], F32, name="ve%d" % h) for h in range(HALVES)]
@@ -94,11 +98,11 @@ def tile_list_engram_dl_tanhL_kernel(
         def product(acc, lhs, lhs_scale, a, start, stop):
             nc.tensor.matmul_mx(
                 out=acc[:], lhsT=lhs, lhsT_scale=lhs_scale,
-                rhs=codes[a][:].bitcast(FP4X4), rhs_scale=planes[a][:], start=start, stop=stop,
+                rhs=codes[:, a, :].bitcast(FP4X4), rhs_scale=planes[a][:], start=start, stop=stop,
             )
 
         def cast(name, a, h, on_vector):
-            grouped = keep.tile([P, P, PACK], BF16, name="grp_%s%d%d" % (name, a, h), align_bytes=64)
+            grouped = keep.tile([P, P, PACK], BF16, name="grp_%s%d%d" % (name, a, h), tag="grp_%s%d%d" % (name, a, h), align_bytes=64)
             dst = grouped[:].rearrange("p (c i) t -> p c t i", i=4)
             src = raw[name, a][:, :, h * P : (h + 1) * P].rearrange("p t (c i) -> p c t i", i=4)
             if on_vector:
@@ -121,34 +125,46 @@ def tile_list_engram_dl_tanhL_kernel(
                 w4scale[:, a, h * P : (h + 1) * P], a, False, stop,
             )
 
-        for name, acc in (("kd", ke), ("v", ve)):
+        quantised = {}
+        for name in ("kd", "v"):
             for a in range(PASSES):
-                grouped = [cast(name, a, h, h == 1 and (name, a) == ("v", 1)) for h in range(HALVES)]
+                grouped = [cast(name, a, h, False) for h in range(HALVES)]
                 if name == "kd":
                     table_pass(a)
-                    if a == 1:
-                        for h in range(HALVES):
-                            base_product(a, h, False)
                 for h in range(HALVES):
-                    wcodes, wscale = quantise(name, a, h, grouped[h])
-                    product(acc[h], wcodes[:].bitcast(FP8X4), wscale[:], a, a == 0, a == PASSES - 1)
-                if name == "kd" and a == 0:
-                    for h in range(HALVES):
-                        base_product(a, h, False)
+                    quantised[name, a, h] = quantise(name, a, h, grouped[h])
+
+        def weight_product(acc, name, a, h, start):
+            wcodes, wscale = quantised[name, a, h]
+            product(acc[h], wcodes[:].bitcast(FP8X4), wscale[:], a, start, not start)
+
+        for h in range(HALVES):
+            weight_product(ke, "kd", 0, h, True)
+            base_product(0, h, False)
+            base_product(1, h, False)
+            weight_product(ke, "kd", 1, h, False)
+        for h in range(HALVES):
+            weight_product(ve, "v", 1, h, True)
+            weight_product(ve, "v", 0, h, False)
 
         gate = []
+        pre = keep.tile([P, HALVES, J], F32, name="pre", tag="raw_v1", align_bytes=64)
         for h in range(HALVES):
-            pre = keep.tile([P, J], F32, name="pre%d" % h, align_bytes=64)
-            nc.vector.tensor_tensor(pre[:], ke[h][:], state[h][:], MULT)
+            nc.vector.tensor_tensor(pre[:, h, :], ke[h][:], state[h][:], MULT)
             gate.append(keep.tile([P, J], F32, name="gate%d" % h, align_bytes=64))
-            nc.scalar.activation(gate[h][:], pre[:], TANH)
+            nc.scalar.activation(gate[h][:], pre[:, h, :], TANH)
+        gated = []
         for h in range(HALVES):
-            gated = keep.tile([P, J], F32, name="gated%d" % h, align_bytes=64)
-            nc.vector.tensor_tensor(gated[:], ve[h][:], gate[h][:], MULT)
-            for c in range(2):
-                cols = slice(c * J // 2, (c + 1) * J // 2)
-                res = keep.tile([P, J // 2], F32, name="res%d%d" % (h, c), align_bytes=64)
+            gated.append(keep.tile([P, J], F32, name="gated%d" % h, align_bytes=64))
+            nc.vector.tensor_tensor(gated[h][:], ve[h][:], gate[h][:], MULT)
+        for h in range(HALVES):
+            pieces = h + 1
+            width = J // pieces
+            for c in range(pieces):
+                cols = slice(c * width, (c + 1) * width)
+                res = keep.tile([P, width], F32, name="res%d%d" % (h, c), tag="raw_v1" if h == 0 else "res%d" % c, align_bytes=64)
                 nc.vector.tensor_tensor(
-                    res[:], record[h][:].indirect(offsets[:, c * J // 32 : (c + 1) * J // 32]), gated[:, cols], ADD
+                    res[:], record[h][:].indirect(offsets[:, c * width // 16 : (c + 1) * width // 16]),
+                    gated[h][:, cols], ADD,
                 )
                 nc.sync.dma_start(out[h * P : (h + 1) * P, cols], res[:])

@@ -23,7 +23,24 @@ PACK = 4
 K_PASS = P * PACK
 PASSES = K // K_PASS
 HALVES = N // P
-QUADS = 4
+QUADRANTS = 4
+QUADRANT = P // QUADRANTS
+SCALE_ROWS = 4
+LIST_ROWS = 16
+ALIGN = 64
+RUN = 4
+
+GPSIMD_CLEARED_WORDS = 320
+GATE_PIECE = J // 2
+LAST_PIECE = 128
+
+
+def load_scale_rows(nc, plane, scales):
+    for quadrant in range(QUADRANTS):
+        nc.sync.dma_start(
+            plane[QUADRANT * quadrant : QUADRANT * quadrant + SCALE_ROWS, :, :].bitcast(I32),
+            scales[:, SCALE_ROWS * quadrant : SCALE_ROWS * (quadrant + 1), :].rearrange("a r c -> r a c").bitcast(I32),
+        )
 
 
 def tile_list_engram_dl_tanhL_kernel(
@@ -35,136 +52,131 @@ def tile_list_engram_dl_tanhL_kernel(
         keep = ctx.enter_context(tc.tile_pool(name="keep", bufs=1))
         psum = ctx.enter_context(tc.psum_pool(name="psum", bufs=1))
 
-        offsets = lists.tile([P, J // 16], U16, name="offsets")
+        def sbuf(shape, dtype, name, slot_of=None):
+            return keep.tile(shape, dtype, name=name, tag=slot_of or name, align_bytes=ALIGN)
+
+        offsets = lists.tile([P, J // LIST_ROWS], U16, name="offsets")
         nc.sync.dma_start(offsets[:], offs)
 
-        tscale = keep.tile([P, PASSES, T], U8, name="tscale", align_bytes=64)
-        cleared = tscale[:].rearrange("p a t -> p (a t)").bitcast(I32)
-        nc.gpsimd.memset(cleared[:, :320], 0)
-        nc.vector.memset(cleared[:, 320:], 0)
-        w4scale = keep.tile([P, PASSES, N], U8, name="w4scale", align_bytes=64)
-        nc.gpsimd.memset(w4scale[:].bitcast(I32), 0)
-        twords = keep.tile([P, T], I32, name="twords", align_bytes=64)
-        nc.sync.dma_start(twords[:], tab_words[0].rearrange("p t b -> p (t b)").bitcast(I32))
-        w4words = keep.tile([P, PASSES, 2 * N], U8, name="w4words", align_bytes=64)
-        nc.sync.dma_start(w4words[:].bitcast(I32), wk4_words.rearrange("a p b -> p a b").bitcast(I32))
-        for q in range(QUADS):
-            nc.sync.dma_start(
-                tscale[32 * q : 32 * q + 4, :, :].bitcast(I32),
-                tab_scales[:, 4 * q : 4 * q + 4, :].rearrange("a r t -> r a t").bitcast(I32),
-            )
+        table_scales = sbuf([P, PASSES, T], U8, "table_scales")
+        cleared = table_scales[:].rearrange("p a t -> p (a t)").bitcast(I32)
+        nc.gpsimd.memset(cleared[:, :GPSIMD_CLEARED_WORDS], 0)
+        nc.vector.memset(cleared[:, GPSIMD_CLEARED_WORDS:], 0)
+        base_scales = sbuf([P, PASSES, N], U8, "base_scales")
+        nc.gpsimd.memset(base_scales[:].bitcast(I32), 0)
+
+        table_words = sbuf([P, T], I32, "table_words")
+        nc.sync.dma_start(table_words[:], tab_words[0].rearrange("p t b -> p (t b)").bitcast(I32))
+        base_words = sbuf([P, PASSES, 2 * N], U8, "base_words")
+        nc.sync.dma_start(base_words[:].bitcast(I32), wk4_words.rearrange("a p b -> p a b").bitcast(I32))
+        load_scale_rows(nc, table_scales, tab_scales)
 
         raw = {}
 
-        def load_weight(name, w, a):
-            raw[name, a] = keep.tile([P, PACK, N], F32, name="raw_%s%d" % (name, a), tag="raw_%s%d" % (name, a), align_bytes=64)
-            nc.sync.dma_start(
-                raw[name, a][:], w[a * K_PASS : (a + 1) * K_PASS, :].rearrange("(p t) n -> p t n", t=PACK)
-            )
+        def load_weight(name, weight, a):
+            raw[name, a] = sbuf([P, PACK, N], F32, "raw_%s%d" % (name, a))
+            rows = weight[a * K_PASS : (a + 1) * K_PASS, :]
+            nc.sync.dma_start(raw[name, a][:], rows.rearrange("(p i) n -> p i n", i=PACK))
 
-        load_weight("kd", wkd, 0)
-        load_weight("kd", wkd, 1)
-        load_weight("v", wv, 0)
-        for q in range(QUADS):
-            nc.sync.dma_start(
-                w4scale[32 * q : 32 * q + 4, :, :].bitcast(I32),
-                wk4_scales[:, 4 * q : 4 * q + 4, :].rearrange("a r n -> r a n").bitcast(I32),
-            )
-        load_weight("v", wv, 1)
+        load_weight("wkd", wkd, 0)
+        load_weight("wkd", wkd, 1)
+        load_weight("wv", wv, 0)
+        load_scale_rows(nc, base_scales, wk4_scales)
+        load_weight("wv", wv, 1)
         state = []
         for h in range(HALVES):
-            state.append(keep.tile([P, J], F32, name="state%d" % h, align_bytes=64))
+            state.append(sbuf([P, J], F32, "state%d" % h))
             nc.sync.dma_start(state[h][:], st[h * P : (h + 1) * P, :])
         record = []
         for h in range(HALVES):
-            record.append(keep.tile([P, T], F32, name="record%d" % h, align_bytes=64))
+            record.append(sbuf([P, T], F32, "record%d" % h))
             nc.sync.dma_start(record[h][:], rT[h * P : (h + 1) * P, :])
 
-        gwords = keep.tile([P, J], U32, name="gwords", align_bytes=64)
-        codes = keep.tile([P, PASSES, J], U16, name="tcodes", align_bytes=64)
-        planes = {}
+        picked_pairs = sbuf([P, J], U32, "picked_pairs")
+        picked_words = sbuf([P, PASSES, J], U16, "picked_words")
+        nc.vector.tensor_copy(picked_pairs[:], table_words[:].bitcast(U32).indirect(offsets[:]))
+        nc.vector.tensor_copy(picked_words[:], picked_pairs[:].bitcast(U16).rearrange("p (j a) -> p a j", a=PASSES))
 
-        def table_pass(a):
-            tag = "raw_kd0" if a == 1 else "gscale0"
-            planes[a] = keep.tile([P, J], U8, name="gscale%d" % a, tag=tag, align_bytes=64)
-            nc.vector.tensor_copy(planes[a][:], tscale[:, a, :].indirect(offsets[:]))
+        picked_scales = {}
 
-        nc.vector.tensor_copy(gwords[:], twords[:].bitcast(U32).indirect(offsets[:]))
-        nc.vector.tensor_copy(codes[:], gwords[:].bitcast(U16).rearrange("p (j d) -> p d j", d=2))
+        def gather_scales(a):
+            slot_of = "raw_wkd0" if a == 1 else None
+            picked_scales[a] = sbuf([P, J], U8, "picked_scales%d" % a, slot_of)
+            nc.vector.tensor_copy(picked_scales[a][:], table_scales[:, a, :].indirect(offsets[:]))
 
         ke = [psum.tile([P, J], F32, name="ke%d" % h) for h in range(HALVES)]
         ve = [psum.tile([P, J], F32, name="ve%d" % h) for h in range(HALVES)]
 
-        def product(acc, lhs, lhs_scale, a, start, stop):
-            nc.tensor.matmul_mx(
-                out=acc[:], lhsT=lhs, lhsT_scale=lhs_scale,
-                rhs=codes[:, a, :].bitcast(FP4X4), rhs_scale=planes[a][:], start=start, stop=stop,
-            )
-
-        def cast(name, a, h, on_vector):
-            grouped = keep.tile([P, P, PACK], BF16, name="grp_%s%d%d" % (name, a, h), tag="grp_%s%d%d" % (name, a, h), align_bytes=64)
-            dst = grouped[:].rearrange("p (c i) t -> p c t i", i=4)
-            src = raw[name, a][:, :, h * P : (h + 1) * P].rearrange("p t (c i) -> p c t i", i=4)
-            if on_vector:
+        def interleave(name, a, h):
+            grouped = sbuf([P, P, PACK], BF16, "grouped_%s%d%d" % (name, a, h))
+            dst = grouped[:].rearrange("p (c r) i -> p c i r", r=RUN)
+            src = raw[name, a][:, :, h * P : (h + 1) * P].rearrange("p i (c r) -> p c i r", r=RUN)
+            if (name, a, h) == ("wv", PASSES - 1, HALVES - 1):
                 nc.vector.tensor_copy(dst, src)
             else:
                 nc.scalar.activation(dst, src, COPY)
             return grouped
 
         def quantise(name, a, h, grouped):
-            wcodes = keep.tile([P, P], U32, name="wc_%s%d%d" % (name, a, h), align_bytes=64)
-            wscale = keep.tile([P, P], U8, name="ws_%s%d%d" % (name, a, h), align_bytes=64)
+            words = sbuf([P, P], U32, "words_%s%d%d" % (name, a, h))
+            scales = sbuf([P, P], U8, "scales_%s%d%d" % (name, a, h))
             nc.vector.quantize_mx(
-                out=wcodes[:].bitcast(FP8X4), scales=wscale[:], in_=grouped[:].rearrange("p n t -> p (n t)")
+                out=words[:].bitcast(FP8X4), scales=scales[:], in_=grouped[:].rearrange("p n i -> p (n i)")
             )
-            return wcodes, wscale
-
-        def base_product(a, h, stop):
-            product(
-                ke[h], w4words[:, a, 2 * P * h : 2 * P * (h + 1)].bitcast(FP4X4),
-                w4scale[:, a, h * P : (h + 1) * P], a, False, stop,
-            )
+            return words, scales
 
         quantised = {}
-        for name in ("kd", "v"):
+        for name in ("wkd", "wv"):
             for a in range(PASSES):
-                grouped = [cast(name, a, h, False) for h in range(HALVES)]
-                if name == "kd":
-                    table_pass(a)
+                grouped_halves = [interleave(name, a, h) for h in range(HALVES)]
+                if name == "wkd":
+                    gather_scales(a)
                 for h in range(HALVES):
-                    quantised[name, a, h] = quantise(name, a, h, grouped[h])
+                    quantised[name, a, h] = quantise(name, a, h, grouped_halves[h])
 
-        def weight_product(acc, name, a, h, start):
-            wcodes, wscale = quantised[name, a, h]
-            product(acc[h], wcodes[:].bitcast(FP8X4), wscale[:], a, start, not start)
+        def product(acc, lhs_words, lhs_scales, a, start, stop):
+            nc.tensor.matmul_mx(
+                out=acc[:],
+                lhsT=lhs_words,
+                lhsT_scale=lhs_scales,
+                rhs=picked_words[:, a, :].bitcast(FP4X4),
+                rhs_scale=picked_scales[a][:],
+                start=start,
+                stop=stop,
+            )
+
+        def weight_product(acc, name, a, h, start, stop):
+            words, scales = quantised[name, a, h]
+            product(acc, words[:].bitcast(FP8X4), scales[:], a, start, stop)
+
+        def base_product(acc, a, h):
+            words = base_words[:, a, 2 * P * h : 2 * P * (h + 1)].bitcast(FP4X4)
+            product(acc, words, base_scales[:, a, h * P : (h + 1) * P], a, False, False)
 
         for h in range(HALVES):
-            weight_product(ke, "kd", 0, h, True)
-            base_product(0, h, False)
-            base_product(1, h, False)
-            weight_product(ke, "kd", 1, h, False)
+            weight_product(ke[h], "wkd", 0, h, True, False)
+            base_product(ke[h], 0, h)
+            base_product(ke[h], 1, h)
+            weight_product(ke[h], "wkd", 1, h, False, True)
         for h in range(HALVES):
-            weight_product(ve, "v", 1, h, True)
-            weight_product(ve, "v", 0, h, False)
+            weight_product(ve[h], "wv", 1, h, True, False)
+            weight_product(ve[h], "wv", 0, h, False, True)
 
         gate = []
-        pre = keep.tile([P, HALVES, J], F32, name="pre", tag="raw_v1", align_bytes=64)
+        gate_input = sbuf([P, HALVES, J], F32, "gate_input", "raw_wv1")
         for h in range(HALVES):
-            nc.vector.tensor_tensor(pre[:, h, :], ke[h][:], state[h][:], MULT)
-            gate.append(keep.tile([P, J], F32, name="gate%d" % h, align_bytes=64))
-            nc.scalar.activation(gate[h][:], pre[:, h, :], TANH)
+            gate.append(sbuf([P, J], F32, "gate%d" % h))
+            for first in range(0, J, GATE_PIECE):
+                cols = slice(first, first + GATE_PIECE)
+                nc.vector.tensor_tensor(gate_input[:, h, cols], ke[h][:, cols], state[h][:, cols], MULT)
+                nc.scalar.activation(gate[h][:, cols], gate_input[:, h, cols], TANH)
         gated = []
         for h in range(HALVES):
-            gated.append(keep.tile([P, J], F32, name="gated%d" % h, align_bytes=64))
+            gated.append(sbuf([P, J], F32, "gated%d" % h))
             nc.vector.tensor_tensor(gated[h][:], ve[h][:], gate[h][:], MULT)
-        for h in range(HALVES):
-            pieces = h + 1
-            width = J // pieces
-            for c in range(pieces):
-                cols = slice(c * width, (c + 1) * width)
-                res = keep.tile([P, width], F32, name="res%d%d" % (h, c), tag="raw_v1" if h == 0 else "res%d" % c, align_bytes=64)
-                nc.vector.tensor_tensor(
-                    res[:], record[h][:].indirect(offsets[:, c * width // 16 : (c + 1) * width // 16]),
-                    gated[h][:, cols], ADD,
-                )
-                nc.sync.dma_start(out[h * P : (h + 1) * P, cols], res[:])
+
+        for h, first, last in ((0, 0, J), (1, 0, J - LAST_PIECE), (1, J - LAST_PIECE, J)):
+            result = sbuf([P, last - first], F32, "result%d_%d" % (h, first), "raw_wv1" if h == 0 else None)
+            picked_record = record[h][:].indirect(offsets[:, first // LIST_ROWS : last // LIST_ROWS])
+            nc.vector.tensor_tensor(result[:], picked_record, gated[h][:, first:last], ADD)
+            nc.sync.dma_start(out[h * P : (h + 1) * P, first:last], result[:])

@@ -68,7 +68,8 @@ def tile_list_engram_dl_tanhL_kernel(
         table_words = sbuf([P, T], I32, "table_words")
         nc.sync.dma_start(table_words[:], tab_words[0].rearrange("p t b -> p (t b)").bitcast(I32))
         base_words = sbuf([P, PASSES, 2 * N], U8, "base_words")
-        nc.sync.dma_start(base_words[:].bitcast(I32), wk4_words.rearrange("a p b -> p a b").bitcast(I32))
+        for a in range(PASSES):
+            nc.sync.dma_start(base_words[:, a, :].bitcast(I32), wk4_words[a].bitcast(I32))
         load_scale_rows(nc, table_scales, tab_scales)
 
         raw = {}
@@ -80,8 +81,8 @@ def tile_list_engram_dl_tanhL_kernel(
 
         load_weight("wkd", wkd, 0)
         load_weight("wkd", wkd, 1)
-        load_weight("wv", wv, 0)
         load_scale_rows(nc, base_scales, wk4_scales)
+        load_weight("wv", wv, 0)
         load_weight("wv", wv, 1)
         state = []
         for h in range(HALVES):
@@ -93,15 +94,16 @@ def tile_list_engram_dl_tanhL_kernel(
             nc.sync.dma_start(record[h][:], rT[h * P : (h + 1) * P, :])
 
         picked_pairs = sbuf([P, J], U32, "picked_pairs")
-        picked_words = sbuf([P, PASSES, J], U16, "picked_words")
         nc.vector.tensor_copy(picked_pairs[:], table_words[:].bitcast(U32).indirect(offsets[:]))
-        nc.vector.tensor_copy(picked_words[:], picked_pairs[:].bitcast(U16).rearrange("p (j a) -> p a j", a=PASSES))
 
+        picked_words = {}
         picked_scales = {}
 
-        def gather_scales(a):
-            slot_of = "raw_wkd0" if a == 1 else None
-            picked_scales[a] = sbuf([P, J], U8, "picked_scales%d" % a, slot_of)
+        def table_operand(a):
+            picked_words[a] = sbuf([P, J], U16, "picked_words%d" % a, "raw_wkd0" if a == 1 else None)
+            words_by_pass = picked_pairs[:].bitcast(U16).rearrange("p (j a) -> p a j", a=PASSES)
+            nc.vector.tensor_copy(picked_words[a][:], words_by_pass[:, a, :])
+            picked_scales[a] = sbuf([P, J], U8, "picked_scales%d" % a, "grouped_wkd01" if a == 1 else None)
             nc.vector.tensor_copy(picked_scales[a][:], table_scales[:, a, :].indirect(offsets[:]))
 
         ke = [psum.tile([P, J], F32, name="ke%d" % h) for h in range(HALVES)]
@@ -130,7 +132,7 @@ def tile_list_engram_dl_tanhL_kernel(
             for a in range(PASSES):
                 grouped_halves = [interleave(name, a, h) for h in range(HALVES)]
                 if name == "wkd":
-                    gather_scales(a)
+                    table_operand(a)
                 for h in range(HALVES):
                     quantised[name, a, h] = quantise(name, a, h, grouped_halves[h])
 
@@ -139,7 +141,7 @@ def tile_list_engram_dl_tanhL_kernel(
                 out=acc[:],
                 lhsT=lhs_words,
                 lhsT_scale=lhs_scales,
-                rhs=picked_words[:, a, :].bitcast(FP4X4),
+                rhs=picked_words[a][:].bitcast(FP4X4),
                 rhs_scale=picked_scales[a][:],
                 start=start,
                 stop=stop,

@@ -36,11 +36,9 @@ LAST_PIECE = 128
 
 
 def load_scale_rows(nc, plane, scales):
-    for quadrant in range(QUADRANTS):
-        nc.sync.dma_start(
-            plane[QUADRANT * quadrant : QUADRANT * quadrant + SCALE_ROWS, :, :].bitcast(I32),
-            scales[:, SCALE_ROWS * quadrant : SCALE_ROWS * (quadrant + 1), :].rearrange("a r c -> r a c").bitcast(I32),
-        )
+    rows = scales.rearrange("a (q r) c -> r q a c", r=SCALE_ROWS)
+    for r in range(SCALE_ROWS):
+        nc.sync.dma_start(plane[r:P:QUADRANT, :, :].bitcast(I32), rows[r].bitcast(I32))
 
 
 def tile_list_engram_dl_tanhL_kernel(

@@ -66,8 +66,7 @@ def tile_list_engram_dl_tanhL_kernel(
         table_words = sbuf([P, T], I32, "table_words")
         nc.sync.dma_start(table_words[:], tab_words[0].rearrange("p t b -> p (t b)").bitcast(I32))
         base_words = sbuf([P, PASSES, 2 * N], U8, "base_words")
-        for a in range(PASSES):
-            nc.sync.dma_start(base_words[:, a, :].bitcast(I32), wk4_words[a].bitcast(I32))
+        nc.sync.dma_start(base_words[:].bitcast(I32), wk4_words.rearrange("a p c -> p a c").bitcast(I32))
         load_scale_rows(nc, table_scales, tab_scales)
 
         raw = {}

@@ -53,6 +53,8 @@ def tile_list_engram_dl_tanhL_kernel(
         def sbuf(shape, dtype, name, slot_of=None):
             return keep.tile(shape, dtype, name=name, tag=slot_of or name, align_bytes=ALIGN)
 
+        table_words = sbuf([P, T], I32, "table_words")
+        nc.sync.dma_start(table_words[:], tab_words[0].rearrange("p t b -> p (t b)").bitcast(I32))
         offsets = lists.tile([P, J // LIST_ROWS], U16, name="offsets")
         nc.sync.dma_start(offsets[:], offs)
 
@@ -63,8 +65,6 @@ def tile_list_engram_dl_tanhL_kernel(
         base_scales = sbuf([P, PASSES, N], U8, "base_scales")
         nc.gpsimd.memset(base_scales[:].bitcast(I32), 0)
 
-        table_words = sbuf([P, T], I32, "table_words")
-        nc.sync.dma_start(table_words[:], tab_words[0].rearrange("p t b -> p (t b)").bitcast(I32))
         base_words = sbuf([P, PASSES, 2 * N], U8, "base_words")
         nc.sync.dma_start(base_words[:].bitcast(I32), wk4_words.rearrange("a p c -> p a c").bitcast(I32))
         load_scale_rows(nc, table_scales, tab_scales)

@@ -32,7 +32,7 @@ RUN = 4
 
 GPSIMD_CLEARED_WORDS = 320
 GATE_PIECE = J // 2
-LAST_PIECE = 128
+LAST_PIECE = 192
 
 
 def load_scale_rows(nc, plane, scales):
@@ -106,32 +106,47 @@ def tile_list_engram_dl_tanhL_kernel(
         ke = [psum.tile([P, J], F32, name="ke%d" % h) for h in range(HALVES)]
         ve = [psum.tile([P, J], F32, name="ve%d" % h) for h in range(HALVES)]
 
-        def interleave(name, a, h):
-            grouped = sbuf([P, P, PACK], BF16, "grouped_%s%d%d" % (name, a, h))
-            dst = grouped[:].rearrange("p (c r) i -> p c i r", r=RUN)
-            src = raw[name, a][:, :, h * P : (h + 1) * P].rearrange("p i (c r) -> p c i r", r=RUN)
-            if (name, a, h) == ("wv", PASSES - 1, HALVES - 1):
-                nc.vector.tensor_copy(dst, src)
-            else:
-                nc.scalar.activation(dst, src, COPY)
-            return grouped
+        def interleave(engine_copy, grouped, name, a, first, width):
+            dst = grouped.rearrange("p (c r) i -> p c i r", r=RUN)
+            src = raw[name, a][:, :, first : first + width].rearrange("p i (c r) -> p c i r", r=RUN)
+            engine_copy(dst, src)
 
-        def quantise(name, a, h, grouped):
-            words = sbuf([P, P], U32, "words_%s%d%d" % (name, a, h))
-            scales = sbuf([P, P], U8, "scales_%s%d%d" % (name, a, h))
+        def scalar_copy(dst, src):
+            nc.scalar.activation(dst, src, COPY)
+
+        gate_inputs = {}
+        quantised = {}
+
+        def quantise(name, a, first, grouped, slot_of=None):
+            width = grouped.shape[1]
+            words = sbuf([P, width], U32, "words_%s%d_%d" % (name, a, first), slot_of)
+            scales = sbuf([P, width], U8, "scales_%s%d_%d" % (name, a, first))
             nc.vector.quantize_mx(
                 out=words[:].bitcast(FP8X4), scales=scales[:], in_=grouped[:].rearrange("p n i -> p (n i)")
             )
-            return words, scales
+            for c in range(0, width, P):
+                quantised[name, a, (first + c) // P] = (words[:, c : c + P], scales[:, c : c + P])
 
-        quantised = {}
-        for name in ("wkd", "wv"):
-            for a in range(PASSES):
-                grouped_halves = [interleave(name, a, h) for h in range(HALVES)]
-                if name == "wkd":
-                    table_operand(a)
-                for h in range(HALVES):
-                    quantised[name, a, h] = quantise(name, a, h, grouped_halves[h])
+        def grouped_tile(name, a, first, width):
+            return sbuf([P, width, PACK], BF16, "grouped_%s%d%d" % (name, a, first // P))
+
+        halves = [grouped_tile("wkd", 0, h * P, P) for h in range(HALVES)]
+        for h in range(HALVES):
+            interleave(scalar_copy, halves[h][:], "wkd", 0, h * P, P)
+        table_operand(0)
+        for h in range(HALVES):
+            quantise("wkd", 0, h * P, halves[h])
+        whole = grouped_tile("wkd", 1, 0, N)
+        interleave(scalar_copy, whole[:], "wkd", 1, 0, N)
+        table_operand(1)
+        quantise("wkd", 1, 0, whole)
+        whole = grouped_tile("wv", 0, 0, N)
+        interleave(scalar_copy, whole[:], "wv", 0, 0, N)
+        halves = [grouped_tile("wv", 1, h * P, P) for h in range(HALVES)]
+        interleave(nc.vector.tensor_copy, halves[0][:], "wv", 1, 0, P)
+        interleave(scalar_copy, halves[1][:], "wv", 1, P, P)
+        quantise("wv", 0, 0, whole)
+        quantise("wv", 1, 0, halves[0])
 
         def product(acc, lhs_words, lhs_scales, a, start, stop):
             nc.tensor.matmul_mx(
@@ -146,36 +161,44 @@ def tile_list_engram_dl_tanhL_kernel(
 
         def weight_product(acc, name, a, h, start, stop):
             words, scales = quantised[name, a, h]
-            product(acc, words[:].bitcast(FP8X4), scales[:], a, start, stop)
+            product(acc, words.bitcast(FP8X4), scales, a, start, stop)
 
-        def base_product(acc, a, h):
+        def base_product(acc, a, h, stop=False):
             words = base_words[:, a, 2 * P * h : 2 * P * (h + 1)].bitcast(FP4X4)
-            product(acc, words, base_scales[:, a, h * P : (h + 1) * P], a, False, False)
+            product(acc, words, base_scales[:, a, h * P : (h + 1) * P], a, False, stop)
 
         for h in range(HALVES):
             weight_product(ke[h], "wkd", 0, h, True, False)
             base_product(ke[h], 0, h)
-            base_product(ke[h], 1, h)
-            weight_product(ke[h], "wkd", 1, h, False, True)
-        for h in range(HALVES):
-            weight_product(ve[h], "wv", 1, h, True, False)
-            weight_product(ve[h], "wv", 0, h, False, True)
+        base_product(ke[0], 1, 0)
+        weight_product(ke[0], "wkd", 1, 0, False, True)
+        weight_product(ke[1], "wkd", 1, 1, False, False)
+        base_product(ke[1], 1, 1, True)
+        def value_product(h):
+            weight_product(ve[h], "wv", 1 - h, h, True, False)
+            weight_product(ve[h], "wv", h, h, False, True)
+
+        value_product(0)
 
         gate = []
-        gate_input = sbuf([P, HALVES, J], F32, "gate_input", "raw_wv1")
         for h in range(HALVES):
             gate.append(sbuf([P, J], F32, "gate%d" % h))
             for first in range(0, J, GATE_PIECE):
                 cols = slice(first, first + GATE_PIECE)
-                nc.vector.tensor_tensor(gate_input[:, h, cols], ke[h][:, cols], state[h][:, cols], MULT)
-                nc.scalar.activation(gate[h][:, cols], gate_input[:, h, cols], TANH)
+                gate_input = sbuf([P, GATE_PIECE], F32, "gate_input%d_%d" % (h, first))
+                gate_inputs[h, first] = gate_input
+                nc.vector.tensor_tensor(gate_input[:], ke[h][:, cols], state[h][:, cols], MULT)
+                nc.scalar.activation(gate[h][:, cols], gate_input[:], TANH)
+            if h == 0:
+                quantise("wv", 1, P, halves[1], "gate_input0_0")
+                value_product(1)
         gated = []
         for h in range(HALVES):
             gated.append(sbuf([P, J], F32, "gated%d" % h))
             nc.vector.tensor_tensor(gated[h][:], ve[h][:], gate[h][:], MULT)
 
         for h, first, last in ((0, 0, J), (1, 0, J - LAST_PIECE), (1, J - LAST_PIECE, J)):
-            result = sbuf([P, last - first], F32, "result%d_%d" % (h, first), "raw_wv1" if h == 0 else None)
+            result = sbuf([P, last - first], F32, "result%d_%d" % (h, first), "gate_input1_256" if h == 0 else None)
             picked_record = record[h][:].indirect(offsets[:, first // LIST_ROWS : last // LIST_ROWS])
             nc.vector.tensor_tensor(result[:], picked_record, gated[h][:, first:last], ADD)
             nc.sync.dma_start(out[h * P : (h + 1) * P, first:last], result[:])

@@ -65,8 +65,13 @@ def tile_list_engram_dl_tanhL_kernel(
         base_scales = sbuf([P, PASSES, N], U8, "base_scales")
         nc.gpsimd.memset(base_scales[:].bitcast(I32), 0)
 
-        base_words = sbuf([P, PASSES, 2 * N], U8, "base_words")
-        nc.sync.dma_start(base_words[:].bitcast(I32), wk4_words.rearrange("a p c -> p a c").bitcast(I32))
+        base_words = {}
+
+        def load_base_words(a):
+            base_words[a] = sbuf([P, 2 * N], U8, "base_words%d" % a)
+            nc.sync.dma_start(base_words[a][:].bitcast(I32), wk4_words[a].bitcast(I32))
+
+        load_base_words(0)
         load_scale_rows(nc, table_scales, tab_scales)
 
         raw = {}
@@ -81,6 +86,7 @@ def tile_list_engram_dl_tanhL_kernel(
         load_scale_rows(nc, base_scales, wk4_scales)
         load_weight("wv", wv, 0)
         load_weight("wv", wv, 1)
+        load_base_words(1)
         state = []
         for h in range(HALVES):
             state.append(sbuf([P, J], F32, "state%d" % h))
@@ -146,7 +152,8 @@ def tile_list_engram_dl_tanhL_kernel(
         interleave(nc.vector.tensor_copy, halves[0][:], "wv", 1, 0, P)
         interleave(scalar_copy, halves[1][:], "wv", 1, P, P)
         quantise("wv", 0, 0, whole)
-        quantise("wv", 1, 0, halves[0])
+        for h in range(HALVES):
+            quantise("wv", 1, h * P, halves[h])
 
         def product(acc, lhs_words, lhs_scales, a, start, stop):
             nc.tensor.matmul_mx(
@@ -164,21 +171,20 @@ def tile_list_engram_dl_tanhL_kernel(
             product(acc, words.bitcast(FP8X4), scales, a, start, stop)
 
         def base_product(acc, a, h, stop=False):
-            words = base_words[:, a, 2 * P * h : 2 * P * (h + 1)].bitcast(FP4X4)
+            words = base_words[a][:, 2 * P * h : 2 * P * (h + 1)].bitcast(FP4X4)
             product(acc, words, base_scales[:, a, h * P : (h + 1) * P], a, False, stop)
 
+        weight_product(ke[0], "wkd", 0, 0, True, False)
+        base_product(ke[0], 0, 0)
+        weight_product(ke[0], "wkd", 1, 0, False, False)
+        base_product(ke[0], 1, 0, True)
+        weight_product(ke[1], "wkd", 0, 1, True, False)
+        base_product(ke[1], 0, 1)
+        base_product(ke[1], 1, 1)
+        weight_product(ke[1], "wkd", 1, 1, False, True)
         for h in range(HALVES):
-            weight_product(ke[h], "wkd", 0, h, True, False)
-            base_product(ke[h], 0, h)
-        base_product(ke[0], 1, 0)
-        weight_product(ke[0], "wkd", 1, 0, False, True)
-        weight_product(ke[1], "wkd", 1, 1, False, False)
-        base_product(ke[1], 1, 1, True)
-        def value_product(h):
-            weight_product(ve[h], "wv", 1 - h, h, True, False)
-            weight_product(ve[h], "wv", h, h, False, True)
-
-        value_product(0)
+            weight_product(ve[h], "wv", 1, h, True, False)
+            weight_product(ve[h], "wv", 0, h, False, True)
 
         gate = []
         for h in range(HALVES):
@@ -189,9 +195,6 @@ def tile_list_engram_dl_tanhL_kernel(
                 gate_inputs[h, first] = gate_input
                 nc.vector.tensor_tensor(gate_input[:], ke[h][:, cols], state[h][:, cols], MULT)
                 nc.scalar.activation(gate[h][:, cols], gate_input[:], TANH)
-            if h == 0:
-                quantise("wv", 1, P, halves[1], "gate_input0_0")
-                value_product(1)
         gated = []
         for h in range(HALVES):
             gated.append(sbuf([P, J], F32, "gated%d" % h))

@@ -174,6 +174,16 @@ def tile_list_engram_dl_tanhL_kernel(
             words = base_words[a][:, 2 * P * h : 2 * P * (h + 1)].bitcast(FP4X4)
             product(acc, words, base_scales[:, a, h * P : (h + 1) * P], a, False, stop)
 
+        unread = psum.tile([P, J], F32, name="unread")
+        nc.tensor.matmul_mx(
+            out=unread[:],
+            lhsT=base_words[0][:, : 2 * P].bitcast(FP4X4),
+            lhsT_scale=table_scales[:, 0, :P],
+            rhs=picked_words[0][:].bitcast(FP4X4),
+            rhs_scale=table_scales[:, 0, :J],
+            start=True,
+            stop=True,
+        )
         weight_product(ke[0], "wkd", 0, 0, True, False)
         base_product(ke[0], 0, 0)
         weight_product(ke[0], "wkd", 1, 0, False, False)

@@ -30,15 +30,8 @@ LIST_ROWS = 16
 ALIGN = 64
 RUN = 4
 
-GPSIMD_CLEARED_WORDS = 320
 GATE_PIECE = J // 2
 LAST_PIECE = 192
-
-
-def load_scale_rows(nc, plane, scales):
-    rows = scales.rearrange("a (q r) c -> r q a c", r=SCALE_ROWS)
-    for r in range(SCALE_ROWS):
-        nc.sync.dma_start(plane[r:P:QUADRANT, :, :].bitcast(I32), rows[r].bitcast(I32))
 
 
 def tile_list_engram_dl_tanhL_kernel(
@@ -53,61 +46,63 @@ def tile_list_engram_dl_tanhL_kernel(
         def sbuf(shape, dtype, name, slot_of=None):
             return keep.tile(shape, dtype, name=name, tag=slot_of or name, align_bytes=ALIGN)
 
-        table_words = sbuf([P, T], I32, "table_words")
-        nc.sync.dma_start(table_words[:], tab_words[0].rearrange("p t b -> p (t b)").bitcast(I32))
+        table_scales = sbuf([P, T], U8, "table_scales")
+        nc.sync.dma_start(
+            table_scales[:QUADRANT, :].bitcast(I32), tab_scales.rearrange("a b c -> b a c").bitcast(I32)
+        )
         offsets = lists.tile([P, J // LIST_ROWS], U16, name="offsets")
         nc.sync.dma_start(offsets[:], offs)
+        table_words = sbuf([P, T], I32, "table_words")
+        nc.sync.dma_start(table_words[:], tab_words[0].rearrange("p t b -> p (t b)").bitcast(I32))
+        nc.vector.memset(table_scales[QUADRANT : 2 * QUADRANT, :].bitcast(I32), 0)
+        nc.vector.memset(table_scales[2 * QUADRANT :, :].bitcast(I32), 0)
 
-        table_scales = sbuf([P, PASSES, T], U8, "table_scales")
-        cleared = table_scales[:].rearrange("p a t -> p (a t)").bitcast(I32)
-        nc.gpsimd.memset(cleared[:, :GPSIMD_CLEARED_WORDS], 0)
-        nc.vector.memset(cleared[:, GPSIMD_CLEARED_WORDS:], 0)
         base_scales = sbuf([P, PASSES, N], U8, "base_scales")
         nc.gpsimd.memset(base_scales[:].bitcast(I32), 0)
-
-        base_words = {}
-
-        def load_base_words(a):
-            base_words[a] = sbuf([P, 2 * N], U8, "base_words%d" % a)
-            nc.sync.dma_start(base_words[a][:].bitcast(I32), wk4_words[a].bitcast(I32))
-
-        load_base_words(0)
-        load_scale_rows(nc, table_scales, tab_scales)
+        planes = sbuf([P, PASSES, J], U8, "planes")
+        nc.gpsimd.memset(planes[:].bitcast(I32), 0)
+        rows = wk4_scales.rearrange("a (q r) c -> r q a c", r=SCALE_ROWS)
+        for r in range(SCALE_ROWS):
+            nc.sync.dma_start(base_scales[r:P:QUADRANT, :, :].bitcast(I32), rows[r].bitcast(I32))
 
         raw = {}
 
-        def load_weight(name, weight, a):
-            raw[name, a] = sbuf([P, PACK, N], F32, "raw_%s%d" % (name, a))
+        def load_weight(name, weight, a, dst):
+            raw[name, a] = dst.rearrange("p (i n) -> p i n", i=PACK)
             rows = weight[a * K_PASS : (a + 1) * K_PASS, :]
-            nc.sync.dma_start(raw[name, a][:], rows.rearrange("(p i) n -> p i n", i=PACK))
+            nc.sync.dma_start(dst, rows.rearrange("(p i) n -> p (i n)", i=PACK))
 
-        load_weight("wkd", wkd, 0)
-        load_weight("wkd", wkd, 1)
-        load_scale_rows(nc, base_scales, wk4_scales)
-        load_weight("wv", wv, 0)
-        load_weight("wv", wv, 1)
-        load_base_words(1)
-        state = []
-        for h in range(HALVES):
-            state.append(sbuf([P, J], F32, "state%d" % h))
-            nc.sync.dma_start(state[h][:], st[h * P : (h + 1) * P, :])
-        record = []
-        for h in range(HALVES):
-            record.append(sbuf([P, T], F32, "record%d" % h))
-            nc.sync.dma_start(record[h][:], rT[h * P : (h + 1) * P, :])
+        for a in range(PASSES):
+            load_weight("wkd", wkd, a, sbuf([P, PACK * N], F32, "raw_wkd%d" % a)[:])
+        base_words = sbuf([P, PASSES, 2 * N], U8, "base_words")
+        nc.sync.dma_start(base_words[:].bitcast(I32), wk4_words.rearrange("a p c -> p a c").bitcast(I32))
 
+        picked_scales = sbuf([P, J], U8, "picked_scales")
+        nc.vector.tensor_copy(picked_scales[:], table_scales[:].indirect(offsets[:]))
+        rows_of_quadrant = PASSES * SCALE_ROWS
+        for q in (0, 2, 1, 3):
+            nc.sync.dma_start(
+                planes[q * QUADRANT : q * QUADRANT + SCALE_ROWS, :, :].bitcast(I32),
+                picked_scales[q * rows_of_quadrant : (q + 1) * rows_of_quadrant, :].bitcast(I32),
+            )
         picked_pairs = sbuf([P, J], U32, "picked_pairs")
         nc.vector.tensor_copy(picked_pairs[:], table_words[:].bitcast(U32).indirect(offsets[:]))
 
-        picked_words = {}
-        picked_scales = {}
+        late = sbuf([P, PASSES * PACK * N + HALVES * J], F32, "late", "table_scales")
+        for a in range(PASSES):
+            load_weight("wv", wv, a, late[:, a * PACK * N : (a + 1) * PACK * N])
+        state = [late[:, PASSES * PACK * N + h * J : PASSES * PACK * N + (h + 1) * J] for h in range(HALVES)]
+        for h in range(HALVES):
+            nc.sync.dma_start(state[h], st[h * P : (h + 1) * P, :])
 
-        def table_operand(a):
-            picked_words[a] = sbuf([P, J], U16, "picked_words%d" % a, "raw_wkd0" if a == 1 else None)
+        picked_words = {}
+
+        def part_words(a, slot_of=None):
+            picked_words[a] = sbuf([P, J], U16, "picked_words%d" % a, slot_of)
             words_by_pass = picked_pairs[:].bitcast(U16).rearrange("p (j a) -> p a j", a=PASSES)
             nc.vector.tensor_copy(picked_words[a][:], words_by_pass[:, a, :])
-            picked_scales[a] = sbuf([P, J], U8, "picked_scales%d" % a, "grouped_wkd01" if a == 1 else None)
-            nc.vector.tensor_copy(picked_scales[a][:], table_scales[:, a, :].indirect(offsets[:]))
+
+        part_words(0)
 
         ke = [psum.tile([P, J], F32, name="ke%d" % h) for h in range(HALVES)]
         ve = [psum.tile([P, J], F32, name="ve%d" % h) for h in range(HALVES)]
@@ -120,12 +115,11 @@ def tile_list_engram_dl_tanhL_kernel(
         def scalar_copy(dst, src):
             nc.scalar.activation(dst, src, COPY)
 
-        gate_inputs = {}
         quantised = {}
 
-        def quantise(name, a, first, grouped, slot_of=None):
+        def quantise(name, a, first, grouped):
             width = grouped.shape[1]
-            words = sbuf([P, width], U32, "words_%s%d_%d" % (name, a, first), slot_of)
+            words = sbuf([P, width], U32, "words_%s%d_%d" % (name, a, first))
             scales = sbuf([P, width], U8, "scales_%s%d_%d" % (name, a, first))
             nc.vector.quantize_mx(
                 out=words[:].bitcast(FP8X4), scales=scales[:], in_=grouped[:].rearrange("p n i -> p (n i)")
@@ -139,19 +133,23 @@ def tile_list_engram_dl_tanhL_kernel(
         halves = [grouped_tile("wkd", 0, h * P, P) for h in range(HALVES)]
         for h in range(HALVES):
             interleave(scalar_copy, halves[h][:], "wkd", 0, h * P, P)
-        table_operand(0)
+        record = [sbuf([P, T], F32, "record0", "table_words"), sbuf([P, T], F32, "record1", "raw_wkd0")]
         for h in range(HALVES):
-            quantise("wkd", 0, h * P, halves[h])
+            nc.sync.dma_start(record[h][:], rT[h * P : (h + 1) * P, :])
+        quantise("wkd", 0, 0, halves[0])
+        part_words(1, "grouped_wkd00")
+        quantise("wkd", 0, P, halves[1])
         whole = grouped_tile("wkd", 1, 0, N)
         interleave(scalar_copy, whole[:], "wkd", 1, 0, N)
-        table_operand(1)
         quantise("wkd", 1, 0, whole)
-        whole = grouped_tile("wv", 0, 0, N)
-        interleave(scalar_copy, whole[:], "wv", 0, 0, N)
+        earlier = [grouped_tile("wv", 0, h * P, P) for h in range(HALVES)]
+        for h in range(HALVES):
+            interleave(scalar_copy, earlier[h][:], "wv", 0, h * P, P)
+        quantise("wv", 0, 0, earlier[0])
         halves = [grouped_tile("wv", 1, h * P, P) for h in range(HALVES)]
         interleave(nc.vector.tensor_copy, halves[0][:], "wv", 1, 0, P)
         interleave(scalar_copy, halves[1][:], "wv", 1, P, P)
-        quantise("wv", 0, 0, whole)
+        quantise("wv", 0, P, earlier[1])
         for h in range(HALVES):
             quantise("wv", 1, h * P, halves[h])
 
@@ -161,7 +159,7 @@ def tile_list_engram_dl_tanhL_kernel(
                 lhsT=lhs_words,
                 lhsT_scale=lhs_scales,
                 rhs=picked_words[a][:].bitcast(FP4X4),
-                rhs_scale=picked_scales[a][:],
+                rhs_scale=planes[:, a, :],
                 start=start,
                 stop=stop,
             )
@@ -170,31 +168,18 @@ def tile_list_engram_dl_tanhL_kernel(
             words, scales = quantised[name, a, h]
             product(acc, words.bitcast(FP8X4), scales, a, start, stop)
 
-        def base_product(acc, a, h, stop=False):
-            words = base_words[a][:, 2 * P * h : 2 * P * (h + 1)].bitcast(FP4X4)
-            product(acc, words, base_scales[:, a, h * P : (h + 1) * P], a, False, stop)
+        def base_product(acc, a, h, start):
+            words = base_words[:, a, 2 * P * h : 2 * P * (h + 1)].bitcast(FP4X4)
+            product(acc, words, base_scales[:, a, h * P : (h + 1) * P], a, start, False)
 
-        unread = psum.tile([P, J], F32, name="unread")
-        nc.tensor.matmul_mx(
-            out=unread[:],
-            lhsT=base_words[0][:, : 2 * P].bitcast(FP4X4),
-            lhsT_scale=table_scales[:, 0, :P],
-            rhs=picked_words[0][:].bitcast(FP4X4),
-            rhs_scale=table_scales[:, 0, :J],
-            start=True,
-            stop=True,
-        )
-        weight_product(ke[0], "wkd", 0, 0, True, False)
-        base_product(ke[0], 0, 0)
-        weight_product(ke[0], "wkd", 1, 0, False, False)
-        base_product(ke[0], 1, 0, True)
-        weight_product(ke[1], "wkd", 0, 1, True, False)
-        base_product(ke[1], 0, 1)
-        base_product(ke[1], 1, 1)
-        weight_product(ke[1], "wkd", 1, 1, False, True)
+        for h, (opening, closing) in enumerate(((0, 1), (1, 0))):
+            weight_product(ke[h], "wkd", opening, h, True, False)
+            base_product(ke[h], 0, h, False)
+            base_product(ke[h], 1, h, False)
+            weight_product(ke[h], "wkd", closing, h, False, True)
         for h in range(HALVES):
-            weight_product(ve[h], "wv", 1, h, True, False)
-            weight_product(ve[h], "wv", 0, h, False, True)
+            weight_product(ve[h], "wv", 0, h, True, False)
+            weight_product(ve[h], "wv", 1, h, False, True)
 
         gate = []
         for h in range(HALVES):
@@ -202,7 +187,6 @@ def tile_list_engram_dl_tanhL_kernel(
             for first in range(0, J, GATE_PIECE):
                 cols = slice(first, first + GATE_PIECE)
                 gate_input = sbuf([P, GATE_PIECE], F32, "gate_input%d_%d" % (h, first))
-                gate_inputs[h, first] = gate_input
                 nc.vector.tensor_tensor(gate_input[:], ke[h][:, cols], state[h][:, cols], MULT)
                 nc.scalar.activation(gate[h][:, cols], gate_input[:], TANH)
         gated = []

@@ -41,13 +41,14 @@ def tile_list_engram_dl_tanhL_kernel(
     with ExitStack() as ctx:
         lists = ctx.enter_context(tc.tile_pool(name="lists", bufs=1))
         keep = ctx.enter_context(tc.tile_pool(name="keep", bufs=1))
+        shared = ctx.enter_context(tc.tile_pool(name="shared", bufs=1))
         psum = ctx.enter_context(tc.psum_pool(name="psum", bufs=1))
 
         def sbuf(shape, dtype, name, slot_of=None):
             return keep.tile(shape, dtype, name=name, tag=slot_of or name, align_bytes=ALIGN)
 
-        table_scales = sbuf([P, T], U8, "table_scales")
-        nc.sync.dma_start(
+        table_scales = shared.tile([P, T], U8, name="table_scales", offset=0, align_bytes=ALIGN)
+        nc.scalar.dma_start(
             table_scales[:QUADRANT, :].bitcast(I32), tab_scales.rearrange("a b c -> b a c").bitcast(I32)
         )
         offsets = lists.tile([P, J // LIST_ROWS], U16, name="offsets")
@@ -74,8 +75,8 @@ def tile_list_engram_dl_tanhL_kernel(
 
         for a in range(PASSES):
             load_weight("wkd", wkd, a, sbuf([P, PACK * N], F32, "raw_wkd%d" % a)[:])
-        base_words = sbuf([P, PASSES, 2 * N], U8, "base_words")
-        nc.sync.dma_start(base_words[:].bitcast(I32), wk4_words.rearrange("a p c -> p a c").bitcast(I32))
+        base_words = [sbuf([P, 2 * N], U8, "base_words0")]
+        nc.sync.dma_start(base_words[0][:].bitcast(I32), wk4_words[0].bitcast(I32))
 
         picked_scales = sbuf([P, J], U8, "picked_scales")
         nc.vector.tensor_copy(picked_scales[:], table_scales[:].indirect(offsets[:]))
@@ -88,9 +89,11 @@ def tile_list_engram_dl_tanhL_kernel(
         picked_pairs = sbuf([P, J], U32, "picked_pairs")
         nc.vector.tensor_copy(picked_pairs[:], table_words[:].bitcast(U32).indirect(offsets[:]))
 
-        late = sbuf([P, PASSES * PACK * N + HALVES * J], F32, "late", "table_scales")
+        late = shared.tile([P, PASSES * PACK * N + HALVES * J], F32, name="late", offset=2 * N, align_bytes=ALIGN)
         for a in range(PASSES):
             load_weight("wv", wv, a, late[:, a * PACK * N : (a + 1) * PACK * N])
+        base_words.append(shared.tile([P, 2 * N], U8, name="base_words1", offset=0, align_bytes=ALIGN))
+        nc.sync.dma_start(base_words[1][:].bitcast(I32), wk4_words[1].bitcast(I32))
         state = [late[:, PASSES * PACK * N + h * J : PASSES * PACK * N + (h + 1) * J] for h in range(HALVES)]
         for h in range(HALVES):
             nc.sync.dma_start(state[h], st[h * P : (h + 1) * P, :])
@@ -168,18 +171,21 @@ def tile_list_engram_dl_tanhL_kernel(
             words, scales = quantised[name, a, h]
             product(acc, words.bitcast(FP8X4), scales, a, start, stop)
 
-        def base_product(acc, a, h, start):
-            words = base_words[:, a, 2 * P * h : 2 * P * (h + 1)].bitcast(FP4X4)
-            product(acc, words, base_scales[:, a, h * P : (h + 1) * P], a, start, False)
+        def base_product(acc, a, h, stop):
+            words = base_words[a][:, 2 * P * h : 2 * P * (h + 1)].bitcast(FP4X4)
+            product(acc, words, base_scales[:, a, h * P : (h + 1) * P], a, False, stop)
 
-        for h, (opening, closing) in enumerate(((0, 1), (1, 0))):
-            weight_product(ke[h], "wkd", opening, h, True, False)
-            base_product(ke[h], 0, h, False)
-            base_product(ke[h], 1, h, False)
-            weight_product(ke[h], "wkd", closing, h, False, True)
+        weight_product(ke[0], "wkd", 0, 0, True, False)
+        base_product(ke[0], 0, 0, False)
+        weight_product(ke[0], "wkd", 1, 0, False, False)
+        base_product(ke[0], 1, 0, True)
+        weight_product(ke[1], "wkd", 0, 1, True, False)
+        base_product(ke[1], 1, 1, False)
+        base_product(ke[1], 0, 1, False)
+        weight_product(ke[1], "wkd", 1, 1, False, True)
         for h in range(HALVES):
-            weight_product(ve[h], "wv", 0, h, True, False)
-            weight_product(ve[h], "wv", 1, h, False, True)
+            weight_product(ve[h], "wv", 1, h, True, False)
+            weight_product(ve[h], "wv", 0, h, False, True)
 
         gate = []
         for h in range(HALVES):

@@ -48,7 +48,7 @@ def tile_list_engram_dl_tanhL_kernel(
             return keep.tile(shape, dtype, name=name, tag=slot_of or name, align_bytes=ALIGN)
 
         table_scales = shared.tile([P, T], U8, name="table_scales", offset=0, align_bytes=ALIGN)
-        nc.scalar.dma_start(
+        nc.sync.dma_start(
             table_scales[:QUADRANT, :].bitcast(I32), tab_scales.rearrange("a b c -> b a c").bitcast(I32)
         )
         offsets = lists.tile([P, J // LIST_ROWS], U16, name="offsets")
@@ -180,8 +180,8 @@ def tile_list_engram_dl_tanhL_kernel(
         weight_product(ke[0], "wkd", 1, 0, False, False)
         base_product(ke[0], 1, 0, True)
         weight_product(ke[1], "wkd", 0, 1, True, False)
-        base_product(ke[1], 1, 1, False)
         base_product(ke[1], 0, 1, False)
+        base_product(ke[1], 1, 1, False)
         weight_product(ke[1], "wkd", 1, 1, False, True)
         for h in range(HALVES):
             weight_product(ve[h], "wv", 1, h, True, False)

@@ -145,16 +145,12 @@ def tile_list_engram_dl_tanhL_kernel(
         whole = grouped_tile("wkd", 1, 0, N)
         interleave(scalar_copy, whole[:], "wkd", 1, 0, N)
         quantise("wkd", 1, 0, whole)
-        earlier = [grouped_tile("wv", 0, h * P, P) for h in range(HALVES)]
-        for h in range(HALVES):
-            interleave(scalar_copy, earlier[h][:], "wv", 0, h * P, P)
-        quantise("wv", 0, 0, earlier[0])
-        halves = [grouped_tile("wv", 1, h * P, P) for h in range(HALVES)]
-        interleave(nc.vector.tensor_copy, halves[0][:], "wv", 1, 0, P)
-        interleave(scalar_copy, halves[1][:], "wv", 1, P, P)
-        quantise("wv", 0, P, earlier[1])
-        for h in range(HALVES):
-            quantise("wv", 1, h * P, halves[h])
+        for a in range(PASSES):
+            halves = [grouped_tile("wv", a, h * P, P) for h in range(HALVES)]
+            interleave(nc.vector.tensor_copy, halves[0][:], "wv", a, 0, P)
+            interleave(scalar_copy, halves[1][:], "wv", a, P, P)
+            for h in range(HALVES):
+                quantise("wv", a, h * P, halves[h])
 
         def product(acc, lhs_words, lhs_scales, a, start, stop):
             nc.tensor.matmul_mx(

@@ -171,6 +171,17 @@ def tile_list_engram_dl_tanhL_kernel(
             words = base_words[a][:, 2 * P * h : 2 * P * (h + 1)].bitcast(FP4X4)
             product(acc, words, base_scales[:, a, h * P : (h + 1) * P], a, False, stop)
 
+        unread = psum.tile([P, J], F32, name="unread")
+        first_words, first_scales = quantised["wkd", 0, 0]
+        nc.tensor.matmul_mx(
+            out=unread[:],
+            lhsT=first_words.bitcast(FP8X4),
+            lhsT_scale=first_scales,
+            rhs=picked_words[0][:].bitcast(FP4X4),
+            rhs_scale=picked_scales[:],
+            start=True,
+            stop=True,
+        )
         weight_product(ke[0], "wkd", 0, 0, True, False)
         base_product(ke[0], 0, 0, False)
         weight_product(ke[0], "wkd", 1, 0, False, False)

from contextlib import ExitStack

import concourse.mybir as mybir

K, N, T, J = 1024, 256, 1024, 512
FLOPS = 3 * 2 * K * N * J

F32 = mybir.dt.float32
BF16 = mybir.dt.bfloat16
I32 = mybir.dt.int32
U32 = mybir.dt.uint32
U16 = mybir.dt.uint16
U8 = mybir.dt.uint8
FP8X4 = mybir.dt.float8_e4m3fn_x4
FP4X4 = mybir.dt.float4_e2m1fn_x4
MULT = mybir.AluOpType.mult
ADD = mybir.AluOpType.add
COPY = mybir.ActivationFunctionType.Copy
TANH = mybir.ActivationFunctionType.Tanh

P = 128
PACK = 4
K_PASS = P * PACK
PASSES = K // K_PASS
HALVES = N // P
QUADRANTS = 4
QUADRANT = P // QUADRANTS
SCALE_ROWS = 4
LIST_ROWS = 16
ALIGN = 64
RUN = 4

GATE_PIECE = J // 2
LAST_PIECE = 192


def tile_list_engram_dl_tanhL_kernel(
    tc, tab_words, tab_scales, wk4_words, wk4_scales, wkd, wv, st, rT, offs, out
):
    nc = tc.nc
    with ExitStack() as ctx:
        lists = ctx.enter_context(tc.tile_pool(name="lists", bufs=1))
        keep = ctx.enter_context(tc.tile_pool(name="keep", bufs=1))
        shared = ctx.enter_context(tc.tile_pool(name="shared", bufs=1))
        psum = ctx.enter_context(tc.psum_pool(name="psum", bufs=1))

        def sbuf(shape, dtype, name, slot_of=None):
            return keep.tile(shape, dtype, name=name, tag=slot_of or name, align_bytes=ALIGN)

        table_scales = shared.tile([P, T], U8, name="table_scales", offset=0, align_bytes=ALIGN)
        nc.sync.dma_start(
            table_scales[:QUADRANT, :].bitcast(I32), tab_scales.rearrange("a b c -> b a c").bitcast(I32)
        )
        offsets = lists.tile([P, J // LIST_ROWS], U16, name="offsets")
        nc.sync.dma_start(offsets[:], offs)
        table_words = sbuf([P, T], I32, "table_words")
        nc.sync.dma_start(table_words[:], tab_words[0].rearrange("p t b -> p (t b)").bitcast(I32))
        nc.vector.memset(table_scales[QUADRANT : 2 * QUADRANT, :].bitcast(I32), 0)
        nc.vector.memset(table_scales[2 * QUADRANT :, :].bitcast(I32), 0)

        base_scales = sbuf([P, PASSES, N], U8, "base_scales")
        nc.gpsimd.memset(base_scales[:].bitcast(I32), 0)
        planes = sbuf([P, PASSES, J], U8, "planes")
        nc.gpsimd.memset(planes[:].bitcast(I32), 0)
        rows = wk4_scales.rearrange("a (q r) c -> r q a c", r=SCALE_ROWS)
        for r in range(SCALE_ROWS):
            nc.sync.dma_start(base_scales[r:P:QUADRANT, :, :].bitcast(I32), rows[r].bitcast(I32))

        raw = {}

        def load_weight(name, weight, a, dst):
            raw[name, a] = dst.rearrange("p (i n) -> p i n", i=PACK)
            rows = weight[a * K_PASS : (a + 1) * K_PASS, :]
            nc.sync.dma_start(dst, rows.rearrange("(p i) n -> p (i n)", i=PACK))

        for a in range(PASSES):
            load_weight("wkd", wkd, a, sbuf([P, PACK * N], F32, "raw_wkd%d" % a)[:])
        base_words = [sbuf([P, 2 * N], U8, "base_words0")]
        nc.sync.dma_start(base_words[0][:].bitcast(I32), wk4_words[0].bitcast(I32))

        picked_scales = sbuf([P, J], U8, "picked_scales")
        nc.vector.tensor_copy(picked_scales[:], table_scales[:].indirect(offsets[:]))
        rows_of_quadrant = PASSES * SCALE_ROWS
        for q in (0, 2, 1, 3):
            nc.sync.dma_start(
                planes[q * QUADRANT : q * QUADRANT + SCALE_ROWS, :, :].bitcast(I32),
                picked_scales[q * rows_of_quadrant : (q + 1) * rows_of_quadrant, :].bitcast(I32),
            )
        picked_pairs = sbuf([P, J], U32, "picked_pairs")
        nc.vector.tensor_copy(picked_pairs[:], table_words[:].bitcast(U32).indirect(offsets[:]))

        late = shared.tile([P, PASSES * PACK * N + HALVES * J], F32, name="late", offset=2 * N, align_bytes=ALIGN)
        for a in range(PASSES):
            load_weight("wv", wv, a, late[:, a * PACK * N : (a + 1) * PACK * N])
        base_words.append(shared.tile([P, 2 * N], U8, name="base_words1", offset=0, align_bytes=ALIGN))
        nc.sync.dma_start(base_words[1][:].bitcast(I32), wk4_words[1].bitcast(I32))
        state = [late[:, PASSES * PACK * N + h * J : PASSES * PACK * N + (h + 1) * J] for h in range(HALVES)]
        for h in range(HALVES):
            nc.sync.dma_start(state[h], st[h * P : (h + 1) * P, :])

        picked_words = {}

        def part_words(a, slot_of=None):
            picked_words[a] = sbuf([P, J], U16, "picked_words%d" % a, slot_of)
            words_by_pass = picked_pairs[:].bitcast(U16).rearrange("p (j a) -> p a j", a=PASSES)
            nc.vector.tensor_copy(picked_words[a][:], words_by_pass[:, a, :])

        part_words(0)

        ke = [psum.tile([P, J], F32, name="ke%d" % h) for h in range(HALVES)]
        ve = [psum.tile([P, J], F32, name="ve%d" % h) for h in range(HALVES)]

        def interleave(engine_copy, grouped, name, a, first, width):
            dst = grouped.rearrange("p (c r) i -> p c i r", r=RUN)
            src = raw[name, a][:, :, first : first + width].rearrange("p i (c r) -> p c i r", r=RUN)
            engine_copy(dst, src)

        def scalar_copy(dst, src):
            nc.scalar.activation(dst, src, COPY)

        quantised = {}

        def quantise(name, a, first, grouped):
            width = grouped.shape[1]
            words = sbuf([P, width], U32, "words_%s%d_%d" % (name, a, first))
            scales = sbuf([P, width], U8, "scales_%s%d_%d" % (name, a, first))
            nc.vector.quantize_mx(
                out=words[:].bitcast(FP8X4), scales=scales[:], in_=grouped[:].rearrange("p n i -> p (n i)")
            )
            for c in range(0, width, P):
                quantised[name, a, (first + c) // P] = (words[:, c : c + P], scales[:, c : c + P])

        def grouped_tile(name, a, first, width):
            return sbuf([P, width, PACK], BF16, "grouped_%s%d%d" % (name, a, first // P))

        halves = [grouped_tile("wkd", 0, h * P, P) for h in range(HALVES)]
        for h in range(HALVES):
            interleave(scalar_copy, halves[h][:], "wkd", 0, h * P, P)
        record = [sbuf([P, T], F32, "record0", "table_words"), sbuf([P, T], F32, "record1", "raw_wkd0")]
        for h in range(HALVES):
            nc.sync.dma_start(record[h][:], rT[h * P : (h + 1) * P, :])
        quantise("wkd", 0, 0, halves[0])
        part_words(1, "grouped_wkd00")
        quantise("wkd", 0, P, halves[1])
        whole = grouped_tile("wkd", 1, 0, N)
        interleave(scalar_copy, whole[:], "wkd", 1, 0, N)
        quantise("wkd", 1, 0, whole)
        for a in range(PASSES):
            halves = [grouped_tile("wv", a, h * P, P) for h in range(HALVES)]
            interleave(nc.vector.tensor_copy, halves[0][:], "wv", a, 0, P)
            interleave(scalar_copy, halves[1][:], "wv", a, P, P)
            for h in range(HALVES):
                quantise("wv", a, h * P, halves[h])

        def product(acc, lhs_words, lhs_scales, a, start, stop):
            nc.tensor.matmul_mx(
                out=acc[:],
                lhsT=lhs_words,
                lhsT_scale=lhs_scales,
                rhs=picked_words[a][:].bitcast(FP4X4),
                rhs_scale=planes[:, a, :],
                start=start,
                stop=stop,
            )

        def weight_product(acc, name, a, h, start, stop):
            words, scales = quantised[name, a, h]
            product(acc, words.bitcast(FP8X4), scales, a, start, stop)

        def base_product(acc, a, h, stop):
            words = base_words[a][:, 2 * P * h : 2 * P * (h + 1)].bitcast(FP4X4)
            product(acc, words, base_scales[:, a, h * P : (h + 1) * P], a, False, stop)

        unread = psum.tile([P, J], F32, name="unread")
        first_words, first_scales = quantised["wkd", 0, 0]
        nc.tensor.matmul_mx(
            out=unread[:],
            lhsT=first_words.bitcast(FP8X4),
            lhsT_scale=first_scales,
            rhs=picked_words[0][:].bitcast(FP4X4),
            rhs_scale=picked_scales[:],
            start=True,
            stop=True,
        )
        weight_product(ke[0], "wkd", 0, 0, True, False)
        base_product(ke[0], 0, 0, False)
        weight_product(ke[0], "wkd", 1, 0, False, False)
        base_product(ke[0], 1, 0, True)
        weight_product(ke[1], "wkd", 0, 1, True, False)
        base_product(ke[1], 0, 1, False)
        base_product(ke[1], 1, 1, False)
        weight_product(ke[1], "wkd", 1, 1, False, True)
        for h in range(HALVES):
            weight_product(ve[h], "wv", 1, h, True, False)
            weight_product(ve[h], "wv", 0, h, False, True)

        gate = []
        for h in range(HALVES):
            gate.append(sbuf([P, J], F32, "gate%d" % h))
            for first in range(0, J, GATE_PIECE):
                cols = slice(first, first + GATE_PIECE)
                gate_input = sbuf([P, GATE_PIECE], F32, "gate_input%d_%d" % (h, first))
                nc.vector.tensor_tensor(gate_input[:], ke[h][:, cols], state[h][:, cols], MULT)
                nc.scalar.activation(gate[h][:, cols], gate_input[:], TANH)
        gated = []
        for h in range(HALVES):
            gated.append(sbuf([P, J], F32, "gated%d" % h))
            nc.vector.tensor_tensor(gated[h][:], ve[h][:], gate[h][:], MULT)

        for h, first, last in ((0, 0, J), (1, 0, J - LAST_PIECE), (1, J - LAST_PIECE, J)):
            result = sbuf([P, last - first], F32, "result%d_%d" % (h, first), "gate_input1_256" if h == 0 else None)
            picked_record = record[h][:].indirect(offsets[:, first // LIST_ROWS : last // LIST_ROWS])
            nc.vector.tensor_tensor(result[:], picked_record, gated[h][:, first:last], ADD)
            nc.sync.dma_start(out[h * P : (h + 1) * P, first:last], result[:])
